import numpy as np
import ml_dtypes


def mxq(x, axis, fmt="e4m3"):
    dtype, down = {"e4m3": (ml_dtypes.float8_e4m3fn, 7), "e5m2": (ml_dtypes.float8_e5m2, 14)}[fmt]
    v = np.moveaxis(np.asarray(x, np.float32).astype(ml_dtypes.bfloat16).astype(np.float64), axis, -1)
    blocks = v.reshape(v.shape[:-1] + (-1, 32))
    amax = np.abs(blocks).max(-1, keepdims=True)
    byte = np.maximum(np.where(amax > 0, np.frexp(amax)[1] - 1 + 127, 0) - down, 1)
    scale = np.exp2(byte - 127.0)
    codes = (blocks / scale).astype(np.float32).astype(dtype).astype(np.float64)
    return np.moveaxis((codes * scale).reshape(v.shape), -1, axis)


WIDE = False


def mx_kscale(k):
    if not WIDE:
        return np.ones(k)
    levels = np.array([10, -10, 5, -5, 0])
    if k % 512:
        return np.exp2(np.random.permutation(np.resize(levels, k // 32))).repeat(32)
    a = np.empty((k // 512, 16))
    for p in range(k // 512):
        a[p, :8] = np.random.permutation(np.resize(levels, 8))
        for g in range(8):
            far = levels[np.abs(levels - a[p, g]) >= 10]
            a[p, g + 8] = far[np.random.randint(len(far))]
    return np.exp2(a.ravel()).repeat(32)


def f64(x):
    return np.asarray(x).astype(np.float64)


def striped8(idx):
    return np.asarray(idx).reshape(8, -1, 16).transpose(0, 2, 1).reshape(128, -1).astype(np.uint16)


def unstriped8(offs):
    return offs.reshape(8, 16, -1).transpose(0, 2, 1).reshape(8, -1).astype(np.int64)


def pick8(x, idx, run):
    r = np.arange(len(x))
    return x[r[:, None], idx[r % (8 * run) // run]]


E2M1 = np.array([0.0, 0.5, 1.0, 1.5, 2.0, 3.0, 4.0, 6.0, -0.0, -0.5, -1.0, -1.5, -2.0, -3.0, -4.0, -6.0])


def pack_weight(w, fmt):
    k, n = w.shape
    w = f64(np.asarray(w, np.float32).astype(ml_dtypes.bfloat16)).reshape(k // 32, 32, n)
    amax = np.abs(w).max(1)
    if fmt == "e4m3":
        byte = np.frexp(amax)[1] - 1 + 127 - 7
    else:
        mant, ex = np.frexp(amax / 6.0)
        byte = np.where(mant > 0.5, ex, ex - 1) + 127
    byte = np.clip(np.where(amax > 0, byte, 1), 1, 254)
    scaled = (w * np.exp2(127.0 - byte)[:, None, :]).reshape(k, n).astype(np.float32)
    by_word = np.ascontiguousarray(scaled.reshape(k // 512, 128, 4, n).transpose(0, 1, 3, 2))
    if fmt == "e4m3":
        words = by_word.astype(ml_dtypes.float8_e4m3fn).view(np.uint8)
    else:
        c = by_word.astype(ml_dtypes.float4_e2m1fn).view(np.uint8) & 0xF
        words = (c[..., 0::2] | (c[..., 1::2] << 4)).reshape(k // 512, 128, 2 * n)
    return np.ascontiguousarray(words), np.ascontiguousarray(byte.astype(np.uint8).reshape(k // 512, 16, n))


def unpack_weight(words, scales, fmt):
    g, _, n = scales.shape
    words = np.ascontiguousarray(words).reshape(g, 128, n, -1)
    if fmt == "e4m3":
        vals = words.view(ml_dtypes.float8_e4m3fn).astype(np.float64)
    else:
        nib = np.empty((g, 128, n, 4), np.uint8)
        nib[..., 0::2] = words & 0xF
        nib[..., 1::2] = words >> 4
        vals = E2M1[nib]
    vals = vals * np.repeat(np.exp2(scales.astype(np.float64) - 127.0), 8, axis=1)[..., None]
    return vals.transpose(0, 1, 3, 2).reshape(g * 512, n)


D, T, U, X, S, I, J, Q = 512, 1024, 1024, 1024, 1024, 512, 256, 128


def setup_inputs():
    n = np.random.standard_normal
    idx = np.stack([np.random.permutation(T)[:J] for _ in range(8)])
    idx2 = np.stack([np.random.permutation(U)[:J] for _ in range(8)])
    idx3 = np.stack([np.random.permutation(X)[:J] for _ in range(8)])
    idx4 = np.stack([np.random.permutation(S)[:J] for _ in range(8)])
    idx5 = np.stack([np.random.permutation(T)[:I] for _ in range(8)])
    idx6 = np.stack([np.random.permutation(U)[:I] for _ in range(8)])
    idx7 = np.stack([np.random.permutation(T)[:I] for _ in range(8)])
    idx8 = np.stack([np.random.permutation(U)[:I] for _ in range(8)])
    fd = mx_kscale(D)
    cachep = pack_weight(n((D, T)) / fd[:, None], "e2m1")
    draftp = pack_weight(n((D, U)) / fd[:, None], "e4m3")
    archp = pack_weight(n((D, X)) / fd[:, None], "e2m1")
    prefp = pack_weight(n((D, S)) / fd[:, None], "e4m3")
    return {
        "query": (n((D, Q)) * 1.0 / np.sqrt(D) * fd[:, None]).astype(np.float32),
        "query2": (n((D, Q)) * 1.0 / np.sqrt(D) * fd[:, None]).astype(np.float32),
        "cache_words": cachep[0],
        "cache_scales": cachep[1],
        "draft_words": draftp[0],
        "draft_scales": draftp[1],
        "arch_words": archp[0],
        "arch_scales": archp[1],
        "pref_words": prefp[0],
        "pref_scales": prefp[1],
        "offs": striped8(idx),
        "offs2": striped8(idx2),
        "offs3": striped8(idx3),
        "offs4": striped8(idx4),
        "offs5": striped8(idx5),
        "offs6": striped8(idx6),
        "offs7": striped8(idx7),
        "offs8": striped8(idx8),
    }


def reference(query, query2, cache_words, cache_scales, draft_words, draft_scales, arch_words, arch_scales, pref_words, pref_scales, offs, offs2, offs3, offs4, offs5, offs6, offs7, offs8):
    idx = unstriped8(offs)
    idx2 = unstriped8(offs2)
    idx3 = unstriped8(offs3)
    idx4 = unstriped8(offs4)
    idx5 = unstriped8(offs5)
    idx6 = unstriped8(offs6)
    idx7 = unstriped8(offs7)
    idx8 = unstriped8(offs8)
    cacheu = unpack_weight(cache_words, cache_scales, "e2m1")
    draftu = unpack_weight(draft_words, draft_scales, "e4m3")
    archu = unpack_weight(arch_words, arch_scales, "e2m1")
    prefu = unpack_weight(pref_words, pref_scales, "e4m3")
    queryq = mxq(f64(query), 0, "e4m3")
    a = queryq.T @ cacheu
    b = queryq.T @ draftu
    query2q = mxq(f64(query2), 0, "e4m3")
    c0 = query2q.T @ archu
    d0 = query2q.T @ prefu
    hi1 = np.maximum(pick8(a, idx, 16), pick8(b, idx2, 16))
    lo1 = np.minimum(pick8(c0, idx3, 16), pick8(d0, idx4, 16))
    w = np.concatenate([hi1, lo1], axis=1)
    f1 = np.zeros((Q, T))
    f1[np.arange(Q)[:, None], idx5[np.arange(Q) % 128 // 16]] = w
    f2 = np.zeros((Q, U))
    f2[np.arange(Q)[:, None], idx6[np.arange(Q) % 128 // 16]] = w
    aa = a - f1
    bb = b + f2
    y = np.minimum(pick8(aa, idx7, 16), pick8(bb, idx8, 16))
    return y

@@ -1,0 +1,200 @@
+from contextlib import ExitStack
+
+import concourse.mybir as mybir
+
+F32 = mybir.dt.float32
+BF16 = mybir.dt.bfloat16
+I32 = mybir.dt.int32
+U32 = mybir.dt.uint32
+U16 = mybir.dt.uint16
+U8 = mybir.dt.uint8
+FP8X4 = mybir.dt.float8_e4m3fn_x4
+FP4X4 = mybir.dt.float4_e2m1fn_x4
+COPY = mybir.ActivationFunctionType.Copy
+ALU = mybir.AluOpType
+
+P = 128
+PACK = 4
+QUADS = 4
+QUAD = 32
+Q = 128
+T = 1024
+PICKS = 256
+SLOTS = 512
+BANK = 512
+LIST_COLS = PICKS // 16
+
+FLOPS = 4 * 2 * 512 * Q * T
+
+
+def tile_attend_fourcourts_fourtwo_kernel(
+    tc, query, query2, cache_words, cache_scales, draft_words, draft_scales,
+    arch_words, arch_scales, pref_words, pref_scales,
+    offs, offs2, offs3, offs4, offs5, offs6, offs7, offs8, out,
+):
+    nc = tc.nc
+    with ExitStack() as ctx:
+        keep = ctx.enter_context(tc.tile_pool(name="keep", bufs=1))
+        psum = ctx.enter_context(tc.psum_pool(name="psum", bufs=1))
+
+        def load_list(src, name):
+            tile = keep.tile(list(src.shape), U16, name=name)
+            nc.sync.dma_start(tile[:], src)
+            return tile
+
+        def load_query(src, name):
+            raw = keep.tile([P, PACK, Q], F32, name=name)
+            nc.sync.dma_start(raw[:], src.rearrange("(p j) w -> p j w", j=PACK))
+            return raw
+
+        def load_scales(tile, row, src, quads):
+            nc.sync.dma_start(
+                tile[row:row + 4, :].bitcast(I32).rearrange("r (g c) -> r g c", g=quads.stop - quads.start),
+                src[0].bitcast(I32).rearrange("(g r) c -> r g c", g=QUADS)[:, quads, :],
+            )
+
+        def spread_scales(tile, rows, home, blocks):
+            words = tile[:].bitcast(I32)
+            width = T // 4
+            for g in range(1, blocks):
+                nc.vector.tensor_copy(
+                    words[home + QUAD * g:home + QUAD * g + rows, 0:width],
+                    words[home:home + rows, g * width:(g + 1) * width],
+                )
+
+        def load_fp4(src, name):
+            tile = keep.tile([P, 2 * T], U8, name=name, align_bytes=256)
+            nc.sync.dma_start(tile[:].bitcast(I32), src[0].bitcast(I32))
+            return tile
+
+        def load_fp8(src, half, name):
+            tile = keep.tile([P, BANK], U32, name=name, align_bytes=256)
+            flat = src[0].rearrange("p n t -> p (n t)").bitcast(I32)
+            nc.sync.dma_start(tile[:].bitcast(I32), flat[:, half * BANK:(half + 1) * BANK])
+            return tile
+
+        def interleave(copy, raw, name):
+            grouped = keep.tile([P, Q, PACK], BF16, name=name, align_bytes=64)
+            copy(
+                grouped[:].rearrange("p (c i) t -> p c t i", i=4),
+                raw[:].rearrange("p t (c i) -> p c t i", i=4),
+            )
+            return grouped
+
+        def quantise(grouped, name):
+            codes = keep.tile([P, Q], U32, name=name + "_codes", align_bytes=64)
+            scales = keep.tile([P, Q], U8, name=name + "_scales", align_bytes=64)
+            nc.vector.quantize_mx(
+                out=codes[:].bitcast(FP8X4), scales=scales[:], in_=grouped[:].rearrange("p w j -> p (w j)")
+            )
+            return codes, scales
+
+        def scores(rows, words, scales, width, tag):
+            bank = psum.tile([P, width], F32, name=tag, tag=tag)
+            nc.tensor.matmul_mx(
+                out=bank[:], lhsT=rows[0][:].bitcast(FP8X4), lhsT_scale=rows[1][:],
+                rhs=words, rhs_scale=scales, start=True, stop=True,
+            )
+            return bank
+
+        cache_plane = keep.tile([P, 2 * T], U8, align_bytes=256)
+        other_planes = keep.tile([P, QUADS * T], U8, align_bytes=256)
+        f1 = keep.tile([P, T], F32)
+        f2 = keep.tile([P, T], F32)
+        nc.vector.memset(cache_plane[:, 0:T].bitcast(I32), 0)
+        nc.vector.memset(other_planes[:].bitcast(I32), 0)
+        nc.vector.memset(f1[:], 0.0)
+        nc.vector.memset(f2[:], 0.0)
+
+        ARCH_ROW, DRAFT_ROW, PREF_ROW = 0, 4, 8
+        q_raw = load_query(query, "q_raw")
+        load_scales(cache_plane, 0, cache_scales, slice(0, 2))
+        load_scales(cache_plane, 2 * QUAD, cache_scales, slice(2, 4))
+        cache = load_fp4(cache_words, "cache")
+        load_scales(other_planes, DRAFT_ROW, draft_scales, slice(0, 4))
+        load_scales(other_planes, ARCH_ROW, arch_scales, slice(0, 4))
+        load_scales(other_planes, PREF_ROW, pref_scales, slice(0, 4))
+        q2_raw = load_query(query2, "q2_raw")
+        draft = [load_fp8(draft_words, h, "draft%d" % h) for h in range(2)]
+        idx = load_list(offs, "idx")
+        idx2 = load_list(offs2, "idx2")
+        arch = load_fp4(arch_words, "arch")
+        idx5 = load_list(offs5, "idx5")
+        pref = [load_fp8(pref_words, h, "pref%d" % h) for h in range(2)]
+        idx6 = load_list(offs6, "idx6")
+        idx3 = load_list(offs3, "idx3")
+        idx4 = load_list(offs4, "idx4")
+        idx7 = load_list(offs7, "idx7")
+        idx8 = load_list(offs8, "idx8")
+
+        a = keep.tile([P, T], F32)
+        b = keep.tile([P, T], F32)
+        c0 = keep.tile([P, T], F32)
+        d0 = keep.tile([P, T], F32)
+        lower, upper = slice(0, BANK), slice(BANK, T)
+
+        q_grouped = interleave(nc.vector.tensor_copy, q_raw, "q_grouped")
+        spread_scales(cache_plane, 4, 0, 2)
+        spread_scales(cache_plane, 4, 2 * QUAD, 2)
+        q_mx = quantise(q_grouped, "q")
+        spread_scales(other_planes, QUAD, 0, QUADS)
+        q2_grouped = interleave(nc.scalar.copy, q2_raw, "q2_grouped")
+
+        a_lo = scores(q_mx, cache[:, 0:T].bitcast(FP4X4), cache_plane[:, lower], BANK, "bank0")
+        a_hi = scores(q_mx, cache[:, T:2 * T].bitcast(FP4X4), cache_plane[:, upper], BANK, "bank1")
+        nc.vector.tensor_copy(a[:, lower], a_lo[:])
+        q2_mx = quantise(q2_grouped, "q2")
+        nc.scalar.copy(a[:, upper], a_hi[:])
+
+        HALF = BANK // 2
+        b_lo = scores(q_mx, draft[0][:].bitcast(FP8X4), other_planes[DRAFT_ROW:P, lower], BANK, "bank2")
+        b_mid = scores(q_mx, draft[1][:, 0:HALF].bitcast(FP8X4), other_planes[DRAFT_ROW:P, BANK:BANK + HALF], HALF, "bank3")
+        b_hi = scores(q_mx, draft[1][:, HALF:BANK].bitcast(FP8X4), other_planes[DRAFT_ROW:P, BANK + HALF:T], HALF, "bank4")
+        nc.vector.tensor_copy(b[:, lower], b_lo[:])
+        nc.scalar.copy(b[:, BANK:BANK + HALF], b_mid[:])
+        pick_a = keep.tile([P, PICKS], F32)
+        nc.scalar.activation(pick_a[:], a[:].indirect(idx[:]), COPY)
+        nc.vector.tensor_copy(b[:, BANK + HALF:T], b_hi[:])
+        pick_b = keep.tile([P, PICKS], F32)
+        nc.vector.tensor_copy(pick_b[:], b[:].indirect(idx2[:]))
+        hi1 = keep.tile([P, PICKS], F32)
+        nc.vector.tensor_tensor(hi1[:], pick_a[:], pick_b[:], ALU.max)
+
+        c_lo = scores(q2_mx, arch[:, 0:T].bitcast(FP4X4), other_planes[:, lower], BANK, "bank5")
+        c_hi = scores(q2_mx, arch[:, T:2 * T].bitcast(FP4X4), other_planes[:, upper], BANK, "bank6")
+        d_lo = scores(q2_mx, pref[0][:].bitcast(FP8X4), other_planes[PREF_ROW:P, lower], BANK, "bank7")
+        d_hi = scores(q2_mx, pref[1][:].bitcast(FP8X4), other_planes[PREF_ROW:P, upper], BANK, "bank0")
+        nc.scalar.copy(c0[:, lower], c_lo[:])
+        nc.scalar.copy(c0[:, upper], c_hi[:])
+
+        first, second = slice(0, LIST_COLS), slice(LIST_COLS, 2 * LIST_COLS)
+        nc.scalar.activation(f1[:].indirect(idx5[:, first]), hi1[:], COPY)
+        nc.scalar.activation(f2[:].indirect(idx6[:, first]), hi1[:], COPY)
+
+        nc.vector.tensor_copy(d0[:, lower], d_lo[:])
+        nc.vector.tensor_copy(d0[:, upper], d_hi[:])
+        pick_c = keep.tile([P, PICKS], F32)
+        nc.vector.tensor_copy(pick_c[:], c0[:].indirect(idx3[:]))
+        pick_d = keep.tile([P, PICKS], F32)
+        nc.vector.tensor_copy(pick_d[:], d0[:].indirect(idx4[:]))
+        lo1 = keep.tile([P, PICKS], F32)
+        nc.vector.tensor_tensor(lo1[:], pick_c[:], pick_d[:], ALU.min)
+
+        nc.scalar.activation(f1[:].indirect(idx5[:, second]), lo1[:], COPY)
+        nc.scalar.activation(f2[:].indirect(idx6[:, second]), lo1[:], COPY)
+
+        aa = keep.tile([P, T], F32)
+        bb = keep.tile([P, T], F32)
+        nc.vector.tensor_tensor(aa[:], a[:], f1[:], ALU.subtract)
+        left = keep.tile([P, SLOTS], F32)
+        nc.scalar.activation(left[:], aa[:].indirect(idx7[:]), COPY)
+        nc.vector.tensor_tensor(bb[:], b[:], f2[:], ALU.add)
+
+        stands = [keep.tile([P, PICKS], F32, name="stands%d" % h) for h in range(2)]
+        nc.vector.tensor_copy(stands[0][:], bb[:].indirect(idx8[:, first]))
+        nc.scalar.activation(stands[1][:], bb[:].indirect(idx8[:, second]), COPY)
+        for h, queue in enumerate((nc.sync, nc.scalar)):
+            cols = slice(h * PICKS, (h + 1) * PICKS)
+            result = keep.tile([P, PICKS], F32, name="result%d" % h)
+            nc.vector.tensor_tensor(result[:], left[:, cols], stands[h][:], ALU.min)
+            queue.dma_start(out[:, cols], result[:])

@@ -100,25 +100,24 @@ def tile_attend_fourcourts_fourtwo_kernel(
         cache_plane = keep.tile([P, 2 * T], U8, align_bytes=256)
         other_planes = keep.tile([P, QUADS * T], U8, align_bytes=256)
         f1 = keep.tile([P, T], F32)
-        f2 = keep.tile([P, T], F32)
         nc.vector.memset(cache_plane[:, 0:T].bitcast(I32), 0)
         nc.vector.memset(other_planes[:].bitcast(I32), 0)
         nc.vector.memset(f1[:], 0.0)
-        nc.vector.memset(f2[:], 0.0)
 
         ARCH_ROW, DRAFT_ROW, PREF_ROW = 0, 4, 8
         q_raw = load_query(query, "q_raw")
         load_scales(cache_plane, 0, cache_scales, slice(0, 2))
         load_scales(cache_plane, 2 * QUAD, cache_scales, slice(2, 4))
         cache = load_fp4(cache_words, "cache")
+        q2_raw = load_query(query2, "q2_raw")
         load_scales(other_planes, DRAFT_ROW, draft_scales, slice(0, 4))
         load_scales(other_planes, ARCH_ROW, arch_scales, slice(0, 4))
         load_scales(other_planes, PREF_ROW, pref_scales, slice(0, 4))
-        q2_raw = load_query(query2, "q2_raw")
-        draft = [load_fp8(draft_words, h, "draft%d" % h) for h in range(2)]
+        draft = [load_fp8(draft_words, 0, "draft0")]
         idx = load_list(offs, "idx")
-        idx2 = load_list(offs2, "idx2")
+        draft.append(load_fp8(draft_words, 1, "draft1"))
         arch = load_fp4(arch_words, "arch")
+        idx2 = load_list(offs2, "idx2")
         idx5 = load_list(offs5, "idx5")
         pref = [load_fp8(pref_words, h, "pref%d" % h) for h in range(2)]
         idx6 = load_list(offs6, "idx6")
@@ -127,7 +126,6 @@ def tile_attend_fourcourts_fourtwo_kernel(
         idx7 = load_list(offs7, "idx7")
         idx8 = load_list(offs8, "idx8")
 
-        a = keep.tile([P, T], F32)
         b = keep.tile([P, T], F32)
         c0 = keep.tile([P, T], F32)
         d0 = keep.tile([P, T], F32)
@@ -137,23 +135,26 @@ def tile_attend_fourcourts_fourtwo_kernel(
         spread_scales(cache_plane, 4, 0, 2)
         spread_scales(cache_plane, 4, 2 * QUAD, 2)
         q_mx = quantise(q_grouped, "q")
-        spread_scales(other_planes, QUAD, 0, QUADS)
         q2_grouped = interleave(nc.scalar.copy, q2_raw, "q2_grouped")
+        spread_scales(other_planes, QUAD, 0, QUADS)
+        q2_mx = quantise(q2_grouped, "q2")
 
+        a = keep.tile([P, T], F32, tag="q2_raw")
         a_lo = scores(q_mx, cache[:, 0:T].bitcast(FP4X4), cache_plane[:, lower], BANK, "bank0")
         a_hi = scores(q_mx, cache[:, T:2 * T].bitcast(FP4X4), cache_plane[:, upper], BANK, "bank1")
-        nc.vector.tensor_copy(a[:, lower], a_lo[:])
-        q2_mx = quantise(q2_grouped, "q2")
+        nc.scalar.copy(a[:, lower], a_lo[:])
         nc.scalar.copy(a[:, upper], a_hi[:])
-
-        HALF = BANK // 2
-        b_lo = scores(q_mx, draft[0][:].bitcast(FP8X4), other_planes[DRAFT_ROW:P, lower], BANK, "bank2")
-        b_mid = scores(q_mx, draft[1][:, 0:HALF].bitcast(FP8X4), other_planes[DRAFT_ROW:P, BANK:BANK + HALF], HALF, "bank3")
-        b_hi = scores(q_mx, draft[1][:, HALF:BANK].bitcast(FP8X4), other_planes[DRAFT_ROW:P, BANK + HALF:T], HALF, "bank4")
-        nc.vector.tensor_copy(b[:, lower], b_lo[:])
-        nc.scalar.copy(b[:, BANK:BANK + HALF], b_mid[:])
         pick_a = keep.tile([P, PICKS], F32)
         nc.scalar.activation(pick_a[:], a[:].indirect(idx[:]), COPY)
+
+        b_lo = scores(q_mx, draft[0][:].bitcast(FP8X4), other_planes[DRAFT_ROW:P, lower], BANK, "bank2")
+        HALF = BANK // 2
+        b_mid = scores(q_mx, draft[1][:, 0:HALF].bitcast(FP8X4), other_planes[DRAFT_ROW:P, BANK:BANK + HALF], HALF, "bank3")
+        b_hi = scores(q_mx, draft[1][:, HALF:BANK].bitcast(FP8X4), other_planes[DRAFT_ROW:P, BANK + HALF:T], HALF, "bank4")
+        f2 = keep.tile([P, T], F32, tag="draft0", align_bytes=256)
+        nc.gpsimd.memset(f2[:], 0.0)
+        nc.vector.tensor_copy(b[:, lower], b_lo[:])
+        nc.scalar.copy(b[:, BANK:BANK + HALF], b_mid[:])
         nc.vector.tensor_copy(b[:, BANK + HALF:T], b_hi[:])
         pick_b = keep.tile([P, PICKS], F32)
         nc.vector.tensor_copy(pick_b[:], b[:].indirect(idx2[:]))

from contextlib import ExitStack

import concourse.mybir as mybir

F32 = mybir.dt.float32
BF16 = mybir.dt.bfloat16
I32 = mybir.dt.int32
U32 = mybir.dt.uint32
U16 = mybir.dt.uint16
U8 = mybir.dt.uint8
FP8X4 = mybir.dt.float8_e4m3fn_x4
FP4X4 = mybir.dt.float4_e2m1fn_x4
COPY = mybir.ActivationFunctionType.Copy
ALU = mybir.AluOpType

P = 128
PACK = 4
QUADS = 4
QUAD = 32
Q = 128
T = 1024
PICKS = 256
SLOTS = 512
BANK = 512
LIST_COLS = PICKS // 16

FLOPS = 4 * 2 * 512 * Q * T


def tile_attend_fourcourts_fourtwo_kernel(
    tc, query, query2, cache_words, cache_scales, draft_words, draft_scales,
    arch_words, arch_scales, pref_words, pref_scales,
    offs, offs2, offs3, offs4, offs5, offs6, offs7, offs8, out,
):
    nc = tc.nc
    with ExitStack() as ctx:
        keep = ctx.enter_context(tc.tile_pool(name="keep", bufs=1))
        psum = ctx.enter_context(tc.psum_pool(name="psum", bufs=1))

        def load_list(src, name):
            tile = keep.tile(list(src.shape), U16, name=name)
            nc.sync.dma_start(tile[:], src)
            return tile

        def load_query(src, name):
            raw = keep.tile([P, PACK, Q], F32, name=name)
            nc.sync.dma_start(raw[:], src.rearrange("(p j) w -> p j w", j=PACK))
            return raw

        def load_scales(tile, row, src, quads):
            nc.sync.dma_start(
                tile[row:row + 4, :].bitcast(I32).rearrange("r (g c) -> r g c", g=quads.stop - quads.start),
                src[0].bitcast(I32).rearrange("(g r) c -> r g c", g=QUADS)[:, quads, :],
            )

        def spread_scales(tile, rows, home, blocks):
            words = tile[:].bitcast(I32)
            width = T // 4
            for g in range(1, blocks):
                nc.vector.tensor_copy(
                    words[home + QUAD * g:home + QUAD * g + rows, 0:width],
                    words[home:home + rows, g * width:(g + 1) * width],
                )

        def load_fp4(src, name):
            tile = keep.tile([P, 2 * T], U8, name=name, align_bytes=256)
            nc.sync.dma_start(tile[:].bitcast(I32), src[0].bitcast(I32))
            return tile

        def load_fp8(src, half, name):
            tile = keep.tile([P, BANK], U32, name=name, align_bytes=256)
            flat = src[0].rearrange("p n t -> p (n t)").bitcast(I32)
            nc.sync.dma_start(tile[:].bitcast(I32), flat[:, half * BANK:(half + 1) * BANK])
            return tile

        def interleave(copy, raw, name):
            grouped = keep.tile([P, Q, PACK], BF16, name=name, align_bytes=64)
            copy(
                grouped[:].rearrange("p (c i) t -> p c t i", i=4),
                raw[:].rearrange("p t (c i) -> p c t i", i=4),
            )
            return grouped

        def quantise(grouped, name):
            codes = keep.tile([P, Q], U32, name=name + "_codes", align_bytes=64)
            scales = keep.tile([P, Q], U8, name=name + "_scales", align_bytes=64)
            nc.vector.quantize_mx(
                out=codes[:].bitcast(FP8X4), scales=scales[:], in_=grouped[:].rearrange("p w j -> p (w j)")
            )
            return codes, scales

        def scores(rows, words, scales, width, tag):
            bank = psum.tile([P, width], F32, name=tag, tag=tag)
            nc.tensor.matmul_mx(
                out=bank[:], lhsT=rows[0][:].bitcast(FP8X4), lhsT_scale=rows[1][:],
                rhs=words, rhs_scale=scales, start=True, stop=True,
            )
            return bank

        cache_plane = keep.tile([P, 2 * T], U8, align_bytes=256)
        other_planes = keep.tile([P, QUADS * T], U8, align_bytes=256)
        f1 = keep.tile([P, T], F32)
        nc.vector.memset(cache_plane[:, 0:T].bitcast(I32), 0)
        nc.vector.memset(other_planes[:].bitcast(I32), 0)
        nc.vector.memset(f1[:], 0.0)

        ARCH_ROW, DRAFT_ROW, PREF_ROW = 0, 4, 8
        q_raw = load_query(query, "q_raw")
        load_scales(cache_plane, 0, cache_scales, slice(0, 2))
        load_scales(cache_plane, 2 * QUAD, cache_scales, slice(2, 4))
        cache = load_fp4(cache_words, "cache")
        q2_raw = load_query(query2, "q2_raw")
        load_scales(other_planes, DRAFT_ROW, draft_scales, slice(0, 4))
        load_scales(other_planes, ARCH_ROW, arch_scales, slice(0, 4))
        load_scales(other_planes, PREF_ROW, pref_scales, slice(0, 4))
        draft = [load_fp8(draft_words, 0, "draft0")]
        idx = load_list(offs, "idx")
        draft.append(load_fp8(draft_words, 1, "draft1"))
        arch = load_fp4(arch_words, "arch")
        idx2 = load_list(offs2, "idx2")
        idx5 = load_list(offs5, "idx5")
        pref = [load_fp8(pref_words, h, "pref%d" % h) for h in range(2)]
        idx6 = load_list(offs6, "idx6")
        idx3 = load_list(offs3, "idx3")
        idx4 = load_list(offs4, "idx4")
        idx7 = load_list(offs7, "idx7")
        idx8 = load_list(offs8, "idx8")

        b = keep.tile([P, T], F32)
        c0 = keep.tile([P, T], F32)
        d0 = keep.tile([P, T], F32)
        lower, upper = slice(0, BANK), slice(BANK, T)

        q_grouped = interleave(nc.vector.tensor_copy, q_raw, "q_grouped")
        spread_scales(cache_plane, 4, 0, 2)
        spread_scales(cache_plane, 4, 2 * QUAD, 2)
        q_mx = quantise(q_grouped, "q")
        q2_grouped = interleave(nc.scalar.copy, q2_raw, "q2_grouped")
        spread_scales(other_planes, QUAD, 0, QUADS)
        q2_mx = quantise(q2_grouped, "q2")

        a = keep.tile([P, T], F32, tag="q2_raw")
        a_lo = scores(q_mx, cache[:, 0:T].bitcast(FP4X4), cache_plane[:, lower], BANK, "bank0")
        a_hi = scores(q_mx, cache[:, T:2 * T].bitcast(FP4X4), cache_plane[:, upper], BANK, "bank1")
        nc.scalar.copy(a[:, lower], a_lo[:])
        nc.scalar.copy(a[:, upper], a_hi[:])
        pick_a = keep.tile([P, PICKS], F32)
        nc.scalar.activation(pick_a[:], a[:].indirect(idx[:]), COPY)

        b_lo = scores(q_mx, draft[0][:].bitcast(FP8X4), other_planes[DRAFT_ROW:P, lower], BANK, "bank2")
        HALF = BANK // 2
        b_mid = scores(q_mx, draft[1][:, 0:HALF].bitcast(FP8X4), other_planes[DRAFT_ROW:P, BANK:BANK + HALF], HALF, "bank3")
        b_hi = scores(q_mx, draft[1][:, HALF:BANK].bitcast(FP8X4), other_planes[DRAFT_ROW:P, BANK + HALF:T], HALF, "bank4")
        f2 = keep.tile([P, T], F32, tag="draft0", align_bytes=256)
        nc.gpsimd.memset(f2[:], 0.0)
        nc.vector.tensor_copy(b[:, lower], b_lo[:])
        nc.scalar.copy(b[:, BANK:BANK + HALF], b_mid[:])
        nc.vector.tensor_copy(b[:, BANK + HALF:T], b_hi[:])
        pick_b = keep.tile([P, PICKS], F32)
        nc.vector.tensor_copy(pick_b[:], b[:].indirect(idx2[:]))
        hi1 = keep.tile([P, PICKS], F32)
        nc.vector.tensor_tensor(hi1[:], pick_a[:], pick_b[:], ALU.max)

        c_lo = scores(q2_mx, arch[:, 0:T].bitcast(FP4X4), other_planes[:, lower], BANK, "bank5")
        c_hi = scores(q2_mx, arch[:, T:2 * T].bitcast(FP4X4), other_planes[:, upper], BANK, "bank6")
        d_lo = scores(q2_mx, pref[0][:].bitcast(FP8X4), other_planes[PREF_ROW:P, lower], BANK, "bank7")
        d_hi = scores(q2_mx, pref[1][:].bitcast(FP8X4), other_planes[PREF_ROW:P, upper], BANK, "bank0")
        nc.scalar.copy(c0[:, lower], c_lo[:])
        nc.scalar.copy(c0[:, upper], c_hi[:])

        first, second = slice(0, LIST_COLS), slice(LIST_COLS, 2 * LIST_COLS)
        nc.scalar.activation(f1[:].indirect(idx5[:, first]), hi1[:], COPY)
        nc.scalar.activation(f2[:].indirect(idx6[:, first]), hi1[:], COPY)

        nc.vector.tensor_copy(d0[:, lower], d_lo[:])
        nc.vector.tensor_copy(d0[:, upper], d_hi[:])
        pick_c = keep.tile([P, PICKS], F32)
        nc.vector.tensor_copy(pick_c[:], c0[:].indirect(idx3[:]))
        pick_d = keep.tile([P, PICKS], F32)
        nc.vector.tensor_copy(pick_d[:], d0[:].indirect(idx4[:]))
        lo1 = keep.tile([P, PICKS], F32)
        nc.vector.tensor_tensor(lo1[:], pick_c[:], pick_d[:], ALU.min)

        nc.scalar.activation(f1[:].indirect(idx5[:, second]), lo1[:], COPY)
        nc.scalar.activation(f2[:].indirect(idx6[:, second]), lo1[:], COPY)

        aa = keep.tile([P, T], F32)
        bb = keep.tile([P, T], F32)
        nc.vector.tensor_tensor(aa[:], a[:], f1[:], ALU.subtract)
        left = keep.tile([P, SLOTS], F32)
        nc.scalar.activation(left[:], aa[:].indirect(idx7[:]), COPY)
        nc.vector.tensor_tensor(bb[:], b[:], f2[:], ALU.add)

        stands = [keep.tile([P, PICKS], F32, name="stands%d" % h) for h in range(2)]
        nc.vector.tensor_copy(stands[0][:], bb[:].indirect(idx8[:, first]))
        nc.scalar.activation(stands[1][:], bb[:].indirect(idx8[:, second]), COPY)
        for h, queue in enumerate((nc.sync, nc.scalar)):
            cols = slice(h * PICKS, (h + 1) * PICKS)
            result = keep.tile([P, PICKS], F32, name="result%d" % h)
            nc.vector.tensor_tensor(result[:], left[:, cols], stands[h][:], ALU.min)
            queue.dma_start(out[:, cols], result[:])
